import numpy as np
import ml_dtypes


def mxq(x, axis, fmt="e4m3"):
    dtype, down = {"e4m3": (ml_dtypes.float8_e4m3fn, 7), "e5m2": (ml_dtypes.float8_e5m2, 14)}[fmt]
    v = np.moveaxis(np.asarray(x, np.float32).astype(ml_dtypes.bfloat16).astype(np.float64), axis, -1)
    blocks = v.reshape(v.shape[:-1] + (-1, 32))
    amax = np.abs(blocks).max(-1, keepdims=True)
    byte = np.maximum(np.where(amax > 0, np.frexp(amax)[1] - 1 + 127, 0) - down, 1)
    scale = np.exp2(byte - 127.0)
    codes = (blocks / scale).astype(np.float32).astype(dtype).astype(np.float64)
    return np.moveaxis((codes * scale).reshape(v.shape), -1, axis)


WIDE = False


def mx_kscale(k):
    if not WIDE:
        return np.ones(k)
    levels = np.array([10, -10, 5, -5, 0])
    if k % 512:
        return np.exp2(np.random.permutation(np.resize(levels, k // 32))).repeat(32)
    a = np.empty((k // 512, 16))
    for p in range(k // 512):
        a[p, :8] = np.random.permutation(np.resize(levels, 8))
        for g in range(8):
            far = levels[np.abs(levels - a[p, g]) >= 10]
            a[p, g + 8] = far[np.random.randint(len(far))]
    return np.exp2(a.ravel()).repeat(32)


def f64(x):
    return np.asarray(x).astype(np.float64)


def striped(idx):
    return np.tile(idx.reshape(-1, 16).T, (8, 1)).astype(np.uint16)


def unstriped(offs):
    return offs[:16].T.reshape(-1).astype(np.int64)


E2M1 = np.array([0.0, 0.5, 1.0, 1.5, 2.0, 3.0, 4.0, 6.0, -0.0, -0.5, -1.0, -1.5, -2.0, -3.0, -4.0, -6.0])


def pack_weight(w, fmt):
    k, n = w.shape
    w = f64(np.asarray(w, np.float32).astype(ml_dtypes.bfloat16)).reshape(k // 32, 32, n)
    amax = np.abs(w).max(1)
    if fmt == "e4m3":
        byte = np.frexp(amax)[1] - 1 + 127 - 7
    else:
        mant, ex = np.frexp(amax / 6.0)
        byte = np.where(mant > 0.5, ex, ex - 1) + 127
    byte = np.clip(np.where(amax > 0, byte, 1), 1, 254)
    scaled = (w * np.exp2(127.0 - byte)[:, None, :]).reshape(k, n).astype(np.float32)
    by_word = np.ascontiguousarray(scaled.reshape(k // 512, 128, 4, n).transpose(0, 1, 3, 2))
    if fmt == "e4m3":
        words = by_word.astype(ml_dtypes.float8_e4m3fn).view(np.uint8)
    else:
        c = by_word.astype(ml_dtypes.float4_e2m1fn).view(np.uint8) & 0xF
        words = (c[..., 0::2] | (c[..., 1::2] << 4)).reshape(k // 512, 128, 2 * n)
    return np.ascontiguousarray(words), np.ascontiguousarray(byte.astype(np.uint8).reshape(k // 512, 16, n))


def unpack_weight(words, scales, fmt):
    g, _, n = scales.shape
    words = np.ascontiguousarray(words).reshape(g, 128, n, -1)
    if fmt == "e4m3":
        vals = words.view(ml_dtypes.float8_e4m3fn).astype(np.float64)
    else:
        nib = np.empty((g, 128, n, 4), np.uint8)
        nib[..., 0::2] = words & 0xF
        nib[..., 1::2] = words >> 4
        vals = E2M1[nib]
    vals = vals * np.repeat(np.exp2(scales.astype(np.float64) - 127.0), 8, axis=1)[..., None]
    return vals.transpose(0, 1, 3, 2).reshape(g * 512, n)


def gelu(v):
    return 0.5 * v * (1.0 + np.tanh(np.sqrt(2.0 / np.pi) * (v + 0.044715 * v**3)))


K, T, H, S, T2, P, N = 1024, 4096, 1024, 1024, 2048, 1024, 512


def setup_inputs():
    n = np.random.standard_normal
    s = mx_kscale(K)[:, None]
    u = mx_kscale(H)[:, None]
    d = {}
    d["tab_words"], d["tab_scales"] = pack_weight(n((K, T)) * s, "e4m3")
    d["offs"] = striped(np.random.permutation(T)[:S])
    d["offs2"] = striped(np.random.permutation(T2)[:S])
    d["offs3"] = striped(np.random.permutation(T2)[:P])
    d["offs4"] = striped(np.random.permutation(T2)[:P])
    d["w1"] = (n((K, H)) * 1.2 / K**0.5 / s).astype(np.float32)
    d["w2_words"], d["w2_scales"] = pack_weight(n((K, H)) * 0.5 / K**0.5 / s, "e4m3")
    d["gain"] = (1.5 * np.exp(0.3 * n(H)) * u[:, 0]).astype(np.float32)
    d["wgs"] = np.exp(0.3 * n((128, S))).astype(np.float32)
    d["page0"] = (n((H, T2)) * u).astype(np.float32)
    d["ref"] = (0.8 * n((H, P)) * u).astype(np.float32)
    d["w3_words"], d["w3_scales"] = pack_weight(n((H, N)) * 0.9 / H**0.5 / u, "e2m1")
    d["wgo"] = np.exp(0.3 * n((128, P))).astype(np.float32)
    d["page1"] = (0.7 * n((N, T2))).astype(np.float32)
    return d


def reference(tab_words, tab_scales, offs, offs2, offs3, offs4, w1, w2_words, w2_scales, gain, wgs, page0, ref, w3_words, w3_scales, wgo, page1):
    v = unpack_weight(tab_words, tab_scales, "e4m3")[:, unstriped(offs)]
    a = mxq(f64(w1), 0, "e4m3").T @ v
    b = unpack_weight(w2_words, w2_scales, "e4m3").T @ v
    h = f64(gain)[:, None] * (1.0 / (1.0 + a * a) + b)
    page = f64(page0).copy()
    page[:, unstriped(offs2)] = np.tile(f64(wgs), (H // 128, 1)) * h
    x = page[:, unstriped(offs3)] - f64(ref)
    xq = mxq(x, 0, "e4m3")
    y = np.tanh(unpack_weight(w3_words, w3_scales, "e2m1").T @ xq)
    out = f64(page1).copy()
    out[:, unstriped(offs4)] = np.tile(f64(wgo), (N // 128, 1)) * y
    return out

@@ -1,0 +1,262 @@
+from contextlib import ExitStack
+
+import concourse.mybir as mybir
+from concourse.masks import make_identity
+
+K, T, H, S, T2, NP, N = 1024, 4096, 1024, 1024, 2048, 1024, 512
+FLOPS = 5368709120
+
+F32 = mybir.dt.float32
+BF16 = mybir.dt.bfloat16
+I32 = mybir.dt.int32
+U32 = mybir.dt.uint32
+U16 = mybir.dt.uint16
+U8 = mybir.dt.uint8
+FP8X4 = mybir.dt.float8_e4m3fn_x4
+FP4X4 = mybir.dt.float4_e2m1fn_x4
+ACT = mybir.ActivationFunctionType
+ALU = mybir.AluOpType
+
+P = 128
+PACK = 4
+PASS = P * PACK
+CHUNK = 256
+HALF = 512
+LIST = 16
+
+
+def tile_list_cask_survey_page_kernel(
+    tc, tab_words, tab_scales, offs, offs2, offs3, offs4, w1, w2_words, w2_scales, gain, wgs, page0, ref,
+    w3_words, w3_scales, wgo, page1, out,
+):
+    nc = tc.nc
+    with ExitStack() as ctx:
+        held = ctx.enter_context(tc.tile_pool(name="held", bufs=1))
+        shared = ctx.enter_context(tc.tile_pool(name="shared", bufs=1))
+        ring = ctx.enter_context(tc.tile_pool(name="ring", bufs=2))
+        psum = ctx.enter_context(tc.psum_pool(name="psum", bufs=4))
+
+        def load_list(name, src):
+            tile = held.tile([P, S // LIST], U16, name=name)
+            nc.sync.dma_start(tile[:], src)
+            return tile
+
+        def cols(lst, start, count):
+            return lst[:, start // LIST : (start + count) // LIST]
+
+        def slot(tag, name, shape, dtype):
+            return held.tile(shape, dtype, name=name, tag=tag, align_bytes=64)
+
+        def interleave(dst, src):
+            nc.scalar.copy(
+                out=dst[:].rearrange("p (c i) t -> p c t i", i=4),
+                in_=src[:].rearrange("p t (c i) -> p c t i", i=4),
+            )
+
+        def ring_rounded(tag):
+            return ring.tile([P, HALF, PACK], BF16, name="rounded", tag=tag, align_bytes=64)
+
+        def quantize(name, src, tag=None):
+            codes = slot(tag or name, name + "_codes", [P, HALF], U32)
+            scales = held.tile([P, HALF], U8, name=name + "_scales", align_bytes=64)
+            nc.vector.quantize_mx(out=codes[:].bitcast(FP8X4), scales=scales[:], in_=src[:].rearrange("p w t -> p (w t)"))
+            return codes, scales
+
+        tabs = slot("tabs", "tabs", [P, T], U8)
+        w2s = held.tile([P, H], U8, name="w2s", align_bytes=64)
+        w3s = held.tile([P, 2, N], U8, name="w3s", align_bytes=64)
+        nc.vector.memset(tabs[:].bitcast(I32), 0)
+        nc.vector.memset(w2s[:].bitcast(I32), 0)
+        nc.vector.memset(w3s[:].rearrange("p a n -> p (a n)").bitcast(I32), 0)
+        ident = held.tile([P, P], F32, name="ident")
+        make_identity(nc, ident[:])
+
+        warm = held.tile([P, 1], F32, name="warm")
+        nc.scalar.activation(warm[:], ident[:, 0:1], ACT.Abs_reciprocal_sqrt, bias=1.0)
+        idx = load_list("idx", offs)
+        tabw = [shared.tile([P, T], U32, name=f"tabw{a}", offset=a * T * 4) for a in range(2)]
+
+        def load_table(a):
+            nc.sync.dma_start(tabw[a][:].bitcast(I32), tab_words[a].rearrange("p t i -> p (t i)").bitcast(I32))
+
+        load_table(0)
+        for q in range(4):
+            nc.scalar.dma_start(tabs[32 * q : 32 * q + 8, :].bitcast(I32), tab_scales[:, 4 * q : 4 * q + 4, :].bitcast(I32))
+        for q in range(4):
+            nc.gpsimd.dma_start(w2s[32 * q : 32 * q + 8, :].bitcast(I32), w2_scales[:, 4 * q : 4 * q + 4, :].bitcast(I32))
+        gains = held.tile([P, 2, PACK], F32, name="gains")
+        nc.gpsimd.dma_start(gains[:], gain.rearrange("(a p t) -> p a t", a=2, t=PACK))
+
+        def load_w1(kp, rp):
+            raw = slot(f"stage{kp}", f"w1raw{kp}{rp}", [P, PACK, HALF], F32)
+            rows = w1[kp * PASS : (kp + 1) * PASS, rp * HALF : (rp + 1) * HALF]
+            nc.sync.dma_start(raw[:], rows.rearrange("(p t) c -> p t c", t=PACK))
+            return raw
+
+        def load_w2(rp):
+            words = held.tile([P, 2, HALF], U32, name=f"w2w{rp}", align_bytes=64)
+            src = w2_words.rearrange("a p c i -> p a (c i)").bitcast(I32)
+            nc.sync.dma_start(words[:].bitcast(I32), src[:, :, rp * HALF : (rp + 1) * HALF])
+            return words
+
+        def quantize_w1(raws, rp):
+            made = []
+            for kp in range(2):
+                rounded = ring_rounded(("resp", "lin")[kp])
+                interleave(rounded, raws[kp])
+                made.append(quantize(f"w1q{kp}{rp}", rounded))
+            return made
+
+        def load_page(rp, t):
+            tile = held.tile([P, T2], F32, name=f"page{rp}{t}")
+            rows = page0[rp * PASS : (rp + 1) * PASS, :].rearrange("(p t) c -> p t c", t=PACK)
+            nc.sync.dma_start(tile[:], rows[:, t, :])
+            return tile
+
+        def load_wgs(name, start, count):
+            tile = held.tile([P, PACK, count], F32, name=name)
+            rows = wgs.rearrange("(c t) j -> c t j", t=PACK)
+            for q in range(4):
+                nc.sync.dma_start(tile[32 * q : 32 * q + 32, :, :], rows[:, :, start : start + count])
+            return tile
+
+        def load_ref(rp, half, tag):
+            tile = slot(tag, f"ref{rp}{half}", [P, PACK, HALF], F32)
+            rows = ref[rp * PASS : (rp + 1) * PASS, half * HALF : (half + 1) * HALF]
+            nc.sync.dma_start(tile[:], rows.rearrange("(p t) m -> p t m", t=PACK))
+            return tile
+
+        w1raw = [load_w1(kp, 0) for kp in range(2)]
+        load_table(1)
+        w2w = [load_w2(0)]
+        idx2 = load_list("idx2", offs2)
+        wgs_parts = {0: load_wgs("wgs_a", 0, CHUNK)}
+        pages = {(0, t): load_page(0, t) for t in range(PACK)}
+        wgs_parts[CHUNK] = load_wgs("wgs_b", CHUNK, CHUNK)
+        wgs_parts[HALF] = load_wgs("wgs_c", HALF, HALF)
+
+        def wgs_cols(t, j0):
+            start = min(j0, HALF)
+            return wgs_parts[start][:, t, j0 - start : j0 - start + CHUNK]
+
+        vw = [slot(tag, f"vw{a}", [P, S], U32) for a, tag in enumerate(("vw0", "tabs"))]
+        vs = held.tile([P, S], U8, name="vs", align_bytes=64)
+        nc.vector.tensor_copy(vw[0][:], tabw[0][:].indirect(idx[:]))
+        nc.vector.tensor_copy(vs[:], tabs[:].indirect(idx[:]))
+        w1q = [quantize_w1(w1raw, 0)]
+        for j0 in range(0, S, HALF):
+            nc.vector.tensor_copy(vw[1][:, j0 : j0 + HALF], tabw[1][:].indirect(cols(idx, j0, HALF)))
+
+        def product(jt, moving):
+            bank = psum.tile([P, HALF], F32, name="bank")
+            js = slice(jt * P, (jt + 1) * P)
+            for kp in range(2):
+                codes, scales = moving[kp]
+                nc.tensor.matmul_mx(
+                    out=bank[:], lhsT=vw[kp][:, js].bitcast(FP8X4), lhsT_scale=vs[4 * kp :, js],
+                    rhs=codes.bitcast(FP8X4), rhs_scale=scales, start=(kp == 0), stop=(kp == 1),
+                )
+            return bank[:].rearrange("j (p t) -> j t p", t=PACK)
+
+        def update(rp, j0, pieces):
+            w1_ops = [(c[:], s[:]) for c, s in w1q[rp]]
+            w2_ops = [(w2w[rp][:, kp, :], w2s[4 * kp :, rp * HALF : (rp + 1) * HALF]) for kp in range(2)]
+            a_banks = [product(j0 // P + u, w1_ops) for u in range(2)]
+            b_banks = [product(j0 // P + u, w2_ops) for u in range(2)]
+            resp = ring.tile([P, PACK, 2, P], F32, name="resp", tag="resp", align_bytes=64)
+            lin = ring.tile([P, PACK, 2, P], F32, name="lin", tag="lin", align_bytes=64)
+            width = PACK // pieces
+            for t0 in range(0, PACK, width):
+                ts = slice(t0, t0 + width)
+                flat = resp[:, ts].rearrange("j t u p -> j (t u p)")
+                for u in range(2):
+                    nc.scalar.activation(resp[:, ts, u, :], a_banks[u][:, ts, :], ACT.Square)
+                nc.scalar.copy(lin[:, ts, 0, :], b_banks[0][:, ts, :])
+                nc.scalar.activation(flat, flat, ACT.Abs_reciprocal_sqrt, bias=1.0)
+                nc.scalar.copy(lin[:, ts, 1, :], b_banks[1][:, ts, :])
+                nc.scalar.activation(flat, flat, ACT.Square)
+                for t in range(t0, t0 + width):
+                    turned = psum.tile([P, CHUNK], F32, name="turned")
+                    h = ring.tile([P, CHUNK], F32, name="h", bufs=12)
+                    for u in range(2):
+                        dst = turned[:, u * P : (u + 1) * P]
+                        nc.tensor.matmul(dst, lhsT=resp[:, t, u, :], rhs=ident[:], is_transpose=True, start=True, stop=False)
+                        nc.tensor.matmul(dst, lhsT=lin[:, t, u, :], rhs=ident[:], is_transpose=True, start=False, stop=True)
+                    nc.scalar.activation(h[:], turned[:], ACT.Copy, scale=gains[:, rp, t : t + 1])
+                    window = pages[rp, t][:].indirect(cols(idx2, j0, CHUNK))
+                    nc.vector.tensor_tensor(window, h[:], wgs_cols(t, j0), ALU.mult)
+
+        def recall(rp, half, refs, tag):
+            diff = slot(tag, f"diff{rp}{half}", [P, PACK, HALF], F32)
+            for t in range(PACK):
+                window = pages[rp, t][:].indirect(cols(idx3, half * HALF, HALF))
+                nc.vector.tensor_tensor(diff[:, t, :], window, refs[:, t, :], ALU.subtract)
+            return diff
+
+        def quantize_x(rp, half, diff, rounded, tag=None):
+            interleave(rounded, diff)
+            return quantize(f"xq{rp}{half}", rounded, tag)
+
+        def score(half, nb, xq, y):
+            bank = psum.tile([P, HALF], F32, name="bank")
+            for rp in range(2):
+                codes, scales = xq[rp]
+                nc.tensor.matmul_mx(
+                    out=bank[:], lhsT=w3w[:, rp, 2 * nb * P : 2 * (nb + 1) * P].bitcast(FP4X4),
+                    lhsT_scale=w3s[:, rp, nb * P : (nb + 1) * P],
+                    rhs=codes[:].bitcast(FP8X4), rhs_scale=scales[:], start=(rp == 0), stop=(rp == 1),
+                )
+            nc.scalar.activation(y, bank[:], ACT.Tanh)
+            window = sheets[nb][:].indirect(cols(idx4, half * HALF, HALF))
+            nc.vector.tensor_tensor(window, y, wgo_sb[:, half * HALF : (half + 1) * HALF], ALU.mult)
+
+        def ring_y():
+            return ring.tile([P, HALF], F32, name="y", bufs=2)[:]
+
+        steps = [(rp, j0) for rp in range(2) for j0 in range(0, S, CHUNK)]
+        xq = {}
+        for i, (rp, j0) in enumerate(steps):
+            if i == 1:
+                w1raw = [load_w1(kp, 1) for kp in range(2)]
+                w2w.append(load_w2(1))
+                idx3 = load_list("idx3", offs3)
+                ref00 = load_ref(0, 0, "stage2")
+                for t in range(PACK):
+                    pages[1, t] = load_page(1, t)
+            if i == 4:
+                w1q.append(quantize_w1(w1raw, 1))
+                ref10 = load_ref(1, 0, "stage0")
+                ref01 = load_ref(0, 1, "stage1")
+                w3w = held.tile([P, 2, 2 * N], U8, name="w3w", align_bytes=64)
+                nc.sync.dma_start(w3w[:].bitcast(I32), w3_words.rearrange("a p c -> p a c").bitcast(I32))
+                for q in range(4):
+                    src = w3_scales[:, 4 * q : 4 * q + 4, :].rearrange("a r n -> r a n")
+                    nc.sync.dma_start(w3s[32 * q : 32 * q + 4, :, :].bitcast(I32), src.bitcast(I32))
+            update(rp, j0, 4 if i == 0 else 1)
+            if i == 4:
+                diff00 = recall(0, 0, ref00, "stage3")
+                ref11 = load_ref(1, 1, "stage2")
+                idx4 = load_list("idx4", offs4)
+                wgo_sb = held.tile([P, NP], F32, name="wgo_sb")
+                nc.sync.dma_start(wgo_sb[:], wgo)
+                sheets = []
+                for nb in range(N // P):
+                    sheet = shared.tile([P, T2], F32, name=f"sheet{nb}", offset=nb * T2 * 4)
+                    nc.sync.dma_start(sheet[:], page1[nb * P : (nb + 1) * P, :])
+                    sheets.append(sheet)
+        xq[0, 0] = quantize_x(0, 0, diff00, ring_rounded("lin"))
+
+        diff10 = recall(1, 0, ref10, "stage3")
+        diff01 = recall(0, 1, ref01, "stage0")
+        xq[1, 0] = quantize_x(1, 0, diff10, slot("stage4", "rounded10", [P, HALF, PACK], BF16), "stage1")
+        diff11 = recall(1, 1, ref11, "stage4")
+        xq[0, 1] = quantize_x(0, 1, diff01, ring_rounded("resp"))
+        score(0, 0, [xq[0, 0], xq[1, 0]], slot("early", "y_early", [P, HALF], F32)[:])
+        score(0, 1, [xq[0, 0], xq[1, 0]], ring_y())
+        xq[1, 1] = quantize_x(1, 1, diff11, ring_rounded("lin"), "early")
+        late = slot("stage4", "y_late", [P, 2, HALF], F32)
+        for nb in range(2, 4):
+            score(0, nb, [xq[0, 0], xq[1, 0]], late[:, nb - 2, :])
+        for nb in range(4):
+            score(1, nb, [xq[0, 1], xq[1, 1]], ring_y())
+            nc.sync.dma_start(out[nb * P : (nb + 1) * P, :], sheets[nb][:])

@@ -33,6 +33,7 @@ def tile_list_cask_survey_page_kernel(
     with ExitStack() as ctx:
         held = ctx.enter_context(tc.tile_pool(name="held", bufs=1))
         shared = ctx.enter_context(tc.tile_pool(name="shared", bufs=1))
+        order = ctx.enter_context(tc.tile_pool(name="order", bufs=1))
         ring = ctx.enter_context(tc.tile_pool(name="ring", bufs=2))
         psum = ctx.enter_context(tc.psum_pool(name="psum", bufs=4))
 
@@ -57,35 +58,40 @@ def tile_list_cask_survey_page_kernel(
             return ring.tile([P, HALF, PACK], BF16, name="rounded", tag=tag, align_bytes=64)
 
         def quantize(name, src, tag=None):
-            codes = slot(tag or name, name + "_codes", [P, HALF], U32)
+            if name == "w1q00":
+                codes = order.tile([P, HALF], U32, name=name + "_codes", offset=0, align_bytes=64)
+            else:
+                codes = slot(tag or name, name + "_codes", [P, HALF], U32)
             scales = held.tile([P, HALF], U8, name=name + "_scales", align_bytes=64)
             nc.vector.quantize_mx(out=codes[:].bitcast(FP8X4), scales=scales[:], in_=src[:].rearrange("p w t -> p (w t)"))
             return codes, scales
 
-        tabs = slot("tabs", "tabs", [P, T], U8)
+        tabs = order.tile([P, T], U8, name="tabs", offset=0, align_bytes=64)
         w2s = held.tile([P, H], U8, name="w2s", align_bytes=64)
         w3s = held.tile([P, 2, N], U8, name="w3s", align_bytes=64)
-        nc.vector.memset(tabs[:].bitcast(I32), 0)
         nc.vector.memset(w2s[:].bitcast(I32), 0)
+        nc.vector.memset(tabs[:].bitcast(I32), 0)
         nc.vector.memset(w3s[:].rearrange("p a n -> p (a n)").bitcast(I32), 0)
         ident = held.tile([P, P], F32, name="ident")
         make_identity(nc, ident[:])
 
         warm = held.tile([P, 1], F32, name="warm")
         nc.scalar.activation(warm[:], ident[:, 0:1], ACT.Abs_reciprocal_sqrt, bias=1.0)
-        idx = load_list("idx", offs)
+        idx, idx2, idx3, idx4 = [load_list(f"idx{i}", src) for i, src in enumerate((offs, offs2, offs3, offs4))]
+        gains = held.tile([P, 2, PACK], F32, name="gains")
+        nc.scalar.dma_start(gains[:], gain.rearrange("(a p t) -> p a t", a=2, t=PACK))
         tabw = [shared.tile([P, T], U32, name=f"tabw{a}", offset=a * T * 4) for a in range(2)]
 
         def load_table(a):
             nc.sync.dma_start(tabw[a][:].bitcast(I32), tab_words[a].rearrange("p t i -> p (t i)").bitcast(I32))
 
+        wgs_rows = slot("stage2", "wgs_rows", [P, HALF], F32)
+        nc.sync.dma_start(wgs_rows[:], wgs[:, :HALF])
         load_table(0)
         for q in range(4):
-            nc.scalar.dma_start(tabs[32 * q : 32 * q + 8, :].bitcast(I32), tab_scales[:, 4 * q : 4 * q + 4, :].bitcast(I32))
+            nc.gpsimd.dma_start(tabs[32 * q : 32 * q + 8, :].bitcast(I32), tab_scales[:, 4 * q : 4 * q + 4, :].bitcast(I32))
         for q in range(4):
-            nc.gpsimd.dma_start(w2s[32 * q : 32 * q + 8, :].bitcast(I32), w2_scales[:, 4 * q : 4 * q + 4, :].bitcast(I32))
-        gains = held.tile([P, 2, PACK], F32, name="gains")
-        nc.gpsimd.dma_start(gains[:], gain.rearrange("(a p t) -> p a t", a=2, t=PACK))
+            nc.scalar.dma_start(w2s[32 * q : 32 * q + 8, :].bitcast(I32), w2_scales[:, 4 * q : 4 * q + 4, :].bitcast(I32))
 
         def load_w1(kp, rp):
             raw = slot(f"stage{kp}", f"w1raw{kp}{rp}", [P, PACK, HALF], F32)
@@ -129,17 +135,26 @@ def tile_list_cask_survey_page_kernel(
         w1raw = [load_w1(kp, 0) for kp in range(2)]
         load_table(1)
         w2w = [load_w2(0)]
-        idx2 = load_list("idx2", offs2)
-        wgs_parts = {0: load_wgs("wgs_a", 0, CHUNK)}
         pages = {(0, t): load_page(0, t) for t in range(PACK)}
-        wgs_parts[CHUNK] = load_wgs("wgs_b", CHUNK, CHUNK)
-        wgs_parts[HALF] = load_wgs("wgs_c", HALF, HALF)
 
-        def wgs_cols(t, j0):
-            start = min(j0, HALF)
-            return wgs_parts[start][:, t, j0 - start : j0 - start + CHUNK]
+        wgs_first = held.tile([P, PACK, HALF], F32, name="wgs_first")
+        wgs_turned = psum.tile([P, PACK, P], F32, name="turned")
+        for u in range(PACK):
+            nc.tensor.transpose(wgs_turned[:, u, :], wgs_rows[:, u * P : (u + 1) * P], ident[:])
+        wgs_spread = slot("stage3", "wgs_spread", [P, PACK, PACK, 4, 32], F32)
+        for q in range(4):
+            nc.vector.tensor_copy(wgs_spread[:, :, :, q, :], wgs_turned[:].rearrange("j u (c t) -> j u t c", t=PACK))
+        for t in range(PACK):
+            back = psum.tile([P, HALF], F32, name="turned")
+            for u in range(PACK):
+                nc.tensor.transpose(back[:, u * P : (u + 1) * P], wgs_spread[:, u, t].rearrange("j q c -> j (q c)"), ident[:])
+            nc.scalar.copy(wgs_first[:, t, :], back[:])
+        wgs_parts = [wgs_first, load_wgs("wgs_second", HALF, HALF)]
 
-        vw = [slot(tag, f"vw{a}", [P, S], U32) for a, tag in enumerate(("vw0", "tabs"))]
+        def wgs_cols(t, j0, count):
+            return wgs_parts[j0 // HALF][:, t, j0 % HALF : j0 % HALF + count]
+
+        vw = [held.tile([P, S], U32, name="vw0", align_bytes=64), order.tile([P, S], U32, name="vw1", offset=HALF * 4, align_bytes=64)]
         vs = held.tile([P, S], U8, name="vs", align_bytes=64)
         nc.vector.tensor_copy(vw[0][:], tabw[0][:].indirect(idx[:]))
         nc.vector.tensor_copy(vs[:], tabs[:].indirect(idx[:]))
@@ -158,7 +173,7 @@ def tile_list_cask_survey_page_kernel(
                 )
             return bank[:].rearrange("j (p t) -> j t p", t=PACK)
 
-        def update(rp, j0, pieces):
+        def update(rp, j0, pieces, span, banks):
             w1_ops = [(c[:], s[:]) for c, s in w1q[rp]]
             w2_ops = [(w2w[rp][:, kp, :], w2s[4 * kp :, rp * HALF : (rp + 1) * HALF]) for kp in range(2)]
             a_banks = [product(j0 // P + u, w1_ops) for u in range(2)]
@@ -176,15 +191,19 @@ def tile_list_cask_survey_page_kernel(
                 nc.scalar.copy(lin[:, ts, 1, :], b_banks[1][:, ts, :])
                 nc.scalar.activation(flat, flat, ACT.Square)
                 for t in range(t0, t0 + width):
-                    turned = psum.tile([P, CHUNK], F32, name="turned")
-                    h = ring.tile([P, CHUNK], F32, name="h", bufs=12)
+                    first = j0 - j0 % span
+                    if j0 == first:
+                        banks[t] = psum.tile([P, span], F32, name="turned")
+                    turned = banks[t]
                     for u in range(2):
-                        dst = turned[:, u * P : (u + 1) * P]
+                        dst = turned[:, j0 - first + u * P : j0 - first + (u + 1) * P]
                         nc.tensor.matmul(dst, lhsT=resp[:, t, u, :], rhs=ident[:], is_transpose=True, start=True, stop=False)
                         nc.tensor.matmul(dst, lhsT=lin[:, t, u, :], rhs=ident[:], is_transpose=True, start=False, stop=True)
-                    nc.scalar.activation(h[:], turned[:], ACT.Copy, scale=gains[:, rp, t : t + 1])
-                    window = pages[rp, t][:].indirect(cols(idx2, j0, CHUNK))
-                    nc.vector.tensor_tensor(window, h[:], wgs_cols(t, j0), ALU.mult)
+                    if j0 + CHUNK == first + span:
+                        h = ring.tile([P, span], F32, name="h", bufs=12)
+                        nc.scalar.activation(h[:], turned[:], ACT.Copy, scale=gains[:, rp, t : t + 1])
+                        window = pages[rp, t][:].indirect(cols(idx2, first, span))
+                        nc.vector.tensor_tensor(window, h[:], wgs_cols(t, first, span), ALU.mult)
 
         def recall(rp, half, refs, tag):
             diff = slot(tag, f"diff{rp}{half}", [P, PACK, HALF], F32)
@@ -208,18 +227,20 @@ def tile_list_cask_survey_page_kernel(
                 )
             nc.scalar.activation(y, bank[:], ACT.Tanh)
             window = sheets[nb][:].indirect(cols(idx4, half * HALF, HALF))
-            nc.vector.tensor_tensor(window, y, wgo_sb[:, half * HALF : (half + 1) * HALF], ALU.mult)
+            z = ring.tile([P, HALF], F32, name="z")
+            nc.vector.tensor_tensor(z[:], y, wgo_sb[:, half * HALF : (half + 1) * HALF], ALU.mult)
+            nc.vector.tensor_copy(window, z[:])
 
         def ring_y():
             return ring.tile([P, HALF], F32, name="y", bufs=2)[:]
 
         steps = [(rp, j0) for rp in range(2) for j0 in range(0, S, CHUNK)]
         xq = {}
+        banks = {}
         for i, (rp, j0) in enumerate(steps):
             if i == 1:
                 w1raw = [load_w1(kp, 1) for kp in range(2)]
                 w2w.append(load_w2(1))
-                idx3 = load_list("idx3", offs3)
                 ref00 = load_ref(0, 0, "stage2")
                 for t in range(PACK):
                     pages[1, t] = load_page(1, t)
@@ -232,11 +253,10 @@ def tile_list_cask_survey_page_kernel(
                 for q in range(4):
                     src = w3_scales[:, 4 * q : 4 * q + 4, :].rearrange("a r n -> r a n")
                     nc.sync.dma_start(w3s[32 * q : 32 * q + 4, :, :].bitcast(I32), src.bitcast(I32))
-            update(rp, j0, 4 if i == 0 else 1)
+            update(rp, j0, 4 if i == 0 else 1, CHUNK, banks)
             if i == 4:
                 diff00 = recall(0, 0, ref00, "stage3")
                 ref11 = load_ref(1, 1, "stage2")
-                idx4 = load_list("idx4", offs4)
                 wgo_sb = held.tile([P, NP], F32, name="wgo_sb")
                 nc.sync.dma_start(wgo_sb[:], wgo)
                 sheets = []

@@ -50,12 +50,12 @@ def tile_list_cask_survey_page_kernel(
 
         def interleave(dst, src):
             nc.scalar.copy(
-                out=dst[:].rearrange("p (c i) t -> p c t i", i=4),
-                in_=src[:].rearrange("p t (c i) -> p c t i", i=4),
+                out=dst.rearrange("p (c i) t -> p c t i", i=4),
+                in_=src.rearrange("p t (c i) -> p c t i", i=4),
             )
 
         def ring_rounded(tag):
-            return ring.tile([P, HALF, PACK], BF16, name="rounded", tag=tag, align_bytes=64)
+            return slot(tag, "rounded", [P, HALF, PACK], BF16)
 
         def quantize(name, src, tag=None):
             if name == "w1q00":
@@ -108,8 +108,8 @@ def tile_list_cask_survey_page_kernel(
         def quantize_w1(raws, rp):
             made = []
             for kp in range(2):
-                rounded = ring_rounded(("resp", "lin")[kp])
-                interleave(rounded, raws[kp])
+                rounded = ring_rounded(("resp", "lin")[kp] + str(1 - rp))
+                interleave(rounded[:], raws[kp][:])
                 made.append(quantize(f"w1q{kp}{rp}", rounded))
             return made
 
@@ -173,48 +173,70 @@ def tile_list_cask_survey_page_kernel(
                 )
             return bank[:].rearrange("j (p t) -> j t p", t=PACK)
 
-        def update(rp, j0, pieces, span, banks):
+        def place(rp, j0, t, turned):
+            h = ring.tile([P, CHUNK], F32, name="h", bufs=12)
+            nc.scalar.activation(h[:], turned[:], ACT.Copy, scale=gains[:, rp, t : t + 1])
+            window = pages[rp, t][:].indirect(cols(idx2, j0, CHUNK))
+            nc.vector.tensor_tensor(window, h[:], wgs_cols(t, j0, CHUNK), ALU.mult)
+
+        def update(step, rp, j0, waiting):
             w1_ops = [(c[:], s[:]) for c, s in w1q[rp]]
             w2_ops = [(w2w[rp][:, kp, :], w2s[4 * kp :, rp * HALF : (rp + 1) * HALF]) for kp in range(2)]
             a_banks = [product(j0 // P + u, w1_ops) for u in range(2)]
             b_banks = [product(j0 // P + u, w2_ops) for u in range(2)]
-            resp = ring.tile([P, PACK, 2, P], F32, name="resp", tag="resp", align_bytes=64)
-            lin = ring.tile([P, PACK, 2, P], F32, name="lin", tag="lin", align_bytes=64)
-            width = PACK // pieces
+            resp = slot(f"resp{step % 2}", "resp", [P, PACK, 2, P], F32)
+            lin = slot(f"lin{step % 2}", "lin", [P, PACK, 2, P], F32)
+            if step < 2:
+                for u in range(2):
+                    nc.vector.tensor_copy(lin[:, :, u, :], b_banks[u])
+            width = (1, 2, 2, 4, 4, 4, 4, 4)[step]
+            left = []
+
+            def place_one():
+                if waiting:
+                    place(*waiting.pop(0))
+
             for t0 in range(0, PACK, width):
                 ts = slice(t0, t0 + width)
                 flat = resp[:, ts].rearrange("j t u p -> j (t u p)")
                 for u in range(2):
                     nc.scalar.activation(resp[:, ts, u, :], a_banks[u][:, ts, :], ACT.Square)
-                nc.scalar.copy(lin[:, ts, 0, :], b_banks[0][:, ts, :])
+                place_one()
+                if step >= 2:
+                    nc.scalar.copy(lin[:, ts, 0, :], b_banks[0][:, ts, :])
+                place_one()
                 nc.scalar.activation(flat, flat, ACT.Abs_reciprocal_sqrt, bias=1.0)
-                nc.scalar.copy(lin[:, ts, 1, :], b_banks[1][:, ts, :])
+                place_one()
+                if step >= 2:
+                    nc.scalar.copy(lin[:, ts, 1, :], b_banks[1][:, ts, :])
+                place_one()
                 nc.scalar.activation(flat, flat, ACT.Square)
                 for t in range(t0, t0 + width):
-                    first = j0 - j0 % span
-                    if j0 == first:
-                        banks[t] = psum.tile([P, span], F32, name="turned")
-                    turned = banks[t]
+                    turned = psum.tile([P, CHUNK], F32, name="turned")
                     for u in range(2):
-                        dst = turned[:, j0 - first + u * P : j0 - first + (u + 1) * P]
+                        dst = turned[:, u * P : (u + 1) * P]
                         nc.tensor.matmul(dst, lhsT=resp[:, t, u, :], rhs=ident[:], is_transpose=True, start=True, stop=False)
                         nc.tensor.matmul(dst, lhsT=lin[:, t, u, :], rhs=ident[:], is_transpose=True, start=False, stop=True)
-                    if j0 + CHUNK == first + span:
-                        h = ring.tile([P, span], F32, name="h", bufs=12)
-                        nc.scalar.activation(h[:], turned[:], ACT.Copy, scale=gains[:, rp, t : t + 1])
-                        window = pages[rp, t][:].indirect(cols(idx2, first, span))
-                        nc.vector.tensor_tensor(window, h[:], wgs_cols(t, first, span), ALU.mult)
+                    if step in (4, 5, 6):
+                        left.append((rp, j0, t, turned))
+                    else:
+                        place(rp, j0, t, turned)
+            return left
 
-        def recall(rp, half, refs, tag):
+        def recall(rp, half, refs, tag, width):
             diff = slot(tag, f"diff{rp}{half}", [P, PACK, HALF], F32)
-            for t in range(PACK):
-                window = pages[rp, t][:].indirect(cols(idx3, half * HALF, HALF))
-                nc.vector.tensor_tensor(diff[:, t, :], window, refs[:, t, :], ALU.subtract)
+            for m0 in range(0, HALF, width):
+                for t in range(PACK):
+                    window = pages[rp, t][:].indirect(cols(idx3, half * HALF + m0, width))
+                    nc.vector.tensor_tensor(diff[:, t, m0 : m0 + width], window, refs[:, t, m0 : m0 + width], ALU.subtract)
             return diff
 
-        def quantize_x(rp, half, diff, rounded, tag=None):
-            interleave(rounded, diff)
-            return quantize(f"xq{rp}{half}", rounded, tag)
+        def quantize_x(name, diff, rounded, width, codes):
+            for m0 in range(0, HALF, width):
+                interleave(rounded[:, m0 : m0 + width, :], diff[:, :, m0 : m0 + width])
+            scales = held.tile([P, HALF], U8, name=name, align_bytes=64)
+            nc.vector.quantize_mx(out=codes.bitcast(FP8X4), scales=scales[:], in_=rounded[:].rearrange("p w t -> p (w t)"))
+            return codes, scales
 
         def score(half, nb, xq, y):
             bank = psum.tile([P, HALF], F32, name="bank")
@@ -223,40 +245,39 @@ def tile_list_cask_survey_page_kernel(
                 nc.tensor.matmul_mx(
                     out=bank[:], lhsT=w3w[:, rp, 2 * nb * P : 2 * (nb + 1) * P].bitcast(FP4X4),
                     lhsT_scale=w3s[:, rp, nb * P : (nb + 1) * P],
-                    rhs=codes[:].bitcast(FP8X4), rhs_scale=scales[:], start=(rp == 0), stop=(rp == 1),
+                    rhs=codes.bitcast(FP8X4), rhs_scale=scales[:], start=(rp == 0), stop=(rp == 1),
                 )
             nc.scalar.activation(y, bank[:], ACT.Tanh)
             window = sheets[nb][:].indirect(cols(idx4, half * HALF, HALF))
-            z = ring.tile([P, HALF], F32, name="z")
-            nc.vector.tensor_tensor(z[:], y, wgo_sb[:, half * HALF : (half + 1) * HALF], ALU.mult)
-            nc.vector.tensor_copy(window, z[:])
+            nc.vector.tensor_tensor(window, y, wgo_sb[:, half * HALF : (half + 1) * HALF], ALU.mult)
 
         def ring_y():
             return ring.tile([P, HALF], F32, name="y", bufs=2)[:]
 
         steps = [(rp, j0) for rp in range(2) for j0 in range(0, S, CHUNK)]
         xq = {}
-        banks = {}
+        waiting = []
         for i, (rp, j0) in enumerate(steps):
             if i == 1:
                 w1raw = [load_w1(kp, 1) for kp in range(2)]
                 w2w.append(load_w2(1))
                 ref00 = load_ref(0, 0, "stage2")
+                ref01 = load_ref(0, 1, "stage4")
                 for t in range(PACK):
                     pages[1, t] = load_page(1, t)
             if i == 4:
                 w1q.append(quantize_w1(w1raw, 1))
                 ref10 = load_ref(1, 0, "stage0")
-                ref01 = load_ref(0, 1, "stage1")
+                ref11 = load_ref(1, 1, "stage1")
                 w3w = held.tile([P, 2, 2 * N], U8, name="w3w", align_bytes=64)
                 nc.sync.dma_start(w3w[:].bitcast(I32), w3_words.rearrange("a p c -> p a c").bitcast(I32))
                 for q in range(4):
                     src = w3_scales[:, 4 * q : 4 * q + 4, :].rearrange("a r n -> r a n")
                     nc.sync.dma_start(w3s[32 * q : 32 * q + 4, :, :].bitcast(I32), src.bitcast(I32))
-            update(rp, j0, 4 if i == 0 else 1, CHUNK, banks)
+            waiting = update(i, rp, j0, waiting)
             if i == 4:
-                diff00 = recall(0, 0, ref00, "stage3")
-                ref11 = load_ref(1, 1, "stage2")
+                diff00 = recall(0, 0, ref00, "stage3", HALF)
+                diff01 = recall(0, 1, ref01, "stage5", HALF)
                 wgo_sb = held.tile([P, NP], F32, name="wgo_sb")
                 nc.sync.dma_start(wgo_sb[:], wgo)
                 sheets = []
@@ -264,16 +285,16 @@ def tile_list_cask_survey_page_kernel(
                     sheet = shared.tile([P, T2], F32, name=f"sheet{nb}", offset=nb * T2 * 4)
                     nc.sync.dma_start(sheet[:], page1[nb * P : (nb + 1) * P, :])
                     sheets.append(sheet)
-        xq[0, 0] = quantize_x(0, 0, diff00, ring_rounded("lin"))
 
-        diff10 = recall(1, 0, ref10, "stage3")
-        diff01 = recall(0, 1, ref01, "stage0")
-        xq[1, 0] = quantize_x(1, 0, diff10, slot("stage4", "rounded10", [P, HALF, PACK], BF16), "stage1")
-        diff11 = recall(1, 1, ref11, "stage4")
-        xq[0, 1] = quantize_x(0, 1, diff01, ring_rounded("resp"))
+        diff10 = recall(1, 0, ref10, "stage2", CHUNK)
+        first_codes = slot("stage0", "first_codes", [P, 2, HALF], U32)
+        xq[0, 0] = quantize_x("xs00", diff00, ring_rounded("lin1"), HALF, first_codes[:, 0, :])
+        xq[0, 1] = quantize_x("xs01", diff01, ring_rounded("resp1"), HALF, first_codes[:, 1, :])
+        xq[1, 0] = quantize_x("xs10", diff10, ring_rounded("stage4"), CHUNK, slot("xq10", "xq10", [P, HALF], U32)[:])
+        diff11 = recall(1, 1, ref11, "stage4", HALF)
         score(0, 0, [xq[0, 0], xq[1, 0]], slot("early", "y_early", [P, HALF], F32)[:])
         score(0, 1, [xq[0, 0], xq[1, 0]], ring_y())
-        xq[1, 1] = quantize_x(1, 1, diff11, ring_rounded("lin"), "early")
+        xq[1, 1] = quantize_x("xs11", diff11, ring_rounded("lin0"), HALF, slot("early", "xq11", [P, HALF], U32)[:])
         late = slot("stage4", "y_late", [P, 2, HALF], F32)
         for nb in range(2, 4):
             score(0, nb, [xq[0, 0], xq[1, 0]], late[:, nb - 2, :])

from contextlib import ExitStack

import concourse.mybir as mybir
from concourse.masks import make_identity

K, T, H, S, T2, NP, N = 1024, 4096, 1024, 1024, 2048, 1024, 512
FLOPS = 5368709120

F32 = mybir.dt.float32
BF16 = mybir.dt.bfloat16
I32 = mybir.dt.int32
U32 = mybir.dt.uint32
U16 = mybir.dt.uint16
U8 = mybir.dt.uint8
FP8X4 = mybir.dt.float8_e4m3fn_x4
FP4X4 = mybir.dt.float4_e2m1fn_x4
ACT = mybir.ActivationFunctionType
ALU = mybir.AluOpType

P = 128
PACK = 4
PASS = P * PACK
CHUNK = 256
HALF = 512
LIST = 16


def tile_list_cask_survey_page_kernel(
    tc, tab_words, tab_scales, offs, offs2, offs3, offs4, w1, w2_words, w2_scales, gain, wgs, page0, ref,
    w3_words, w3_scales, wgo, page1, out,
):
    nc = tc.nc
    with ExitStack() as ctx:
        held = ctx.enter_context(tc.tile_pool(name="held", bufs=1))
        shared = ctx.enter_context(tc.tile_pool(name="shared", bufs=1))
        order = ctx.enter_context(tc.tile_pool(name="order", bufs=1))
        ring = ctx.enter_context(tc.tile_pool(name="ring", bufs=2))
        psum = ctx.enter_context(tc.psum_pool(name="psum", bufs=4))

        def load_list(name, src):
            tile = held.tile([P, S // LIST], U16, name=name)
            nc.sync.dma_start(tile[:], src)
            return tile

        def cols(lst, start, count):
            return lst[:, start // LIST : (start + count) // LIST]

        def slot(tag, name, shape, dtype):
            return held.tile(shape, dtype, name=name, tag=tag, align_bytes=64)

        def interleave(dst, src):
            nc.scalar.copy(
                out=dst.rearrange("p (c i) t -> p c t i", i=4),
                in_=src.rearrange("p t (c i) -> p c t i", i=4),
            )

        def ring_rounded(tag):
            return slot(tag, "rounded", [P, HALF, PACK], BF16)

        def quantize(name, src, tag=None):
            if name == "w1q00":
                codes = order.tile([P, HALF], U32, name=name + "_codes", offset=0, align_bytes=64)
            else:
                codes = slot(tag or name, name + "_codes", [P, HALF], U32)
            scales = held.tile([P, HALF], U8, name=name + "_scales", align_bytes=64)
            nc.vector.quantize_mx(out=codes[:].bitcast(FP8X4), scales=scales[:], in_=src[:].rearrange("p w t -> p (w t)"))
            return codes, scales

        tabs = order.tile([P, T], U8, name="tabs", offset=0, align_bytes=64)
        w2s = held.tile([P, H], U8, name="w2s", align_bytes=64)
        w3s = held.tile([P, 2, N], U8, name="w3s", align_bytes=64)
        nc.vector.memset(w2s[:].bitcast(I32), 0)
        nc.vector.memset(tabs[:].bitcast(I32), 0)
        nc.vector.memset(w3s[:].rearrange("p a n -> p (a n)").bitcast(I32), 0)
        ident = held.tile([P, P], F32, name="ident")
        make_identity(nc, ident[:])

        warm = held.tile([P, 1], F32, name="warm")
        nc.scalar.activation(warm[:], ident[:, 0:1], ACT.Abs_reciprocal_sqrt, bias=1.0)
        idx, idx2, idx3, idx4 = [load_list(f"idx{i}", src) for i, src in enumerate((offs, offs2, offs3, offs4))]
        gains = held.tile([P, 2, PACK], F32, name="gains")
        nc.scalar.dma_start(gains[:], gain.rearrange("(a p t) -> p a t", a=2, t=PACK))
        tabw = [shared.tile([P, T], U32, name=f"tabw{a}", offset=a * T * 4) for a in range(2)]

        def load_table(a):
            nc.sync.dma_start(tabw[a][:].bitcast(I32), tab_words[a].rearrange("p t i -> p (t i)").bitcast(I32))

        wgs_rows = slot("stage2", "wgs_rows", [P, HALF], F32)
        nc.sync.dma_start(wgs_rows[:], wgs[:, :HALF])
        load_table(0)
        for q in range(4):
            nc.gpsimd.dma_start(tabs[32 * q : 32 * q + 8, :].bitcast(I32), tab_scales[:, 4 * q : 4 * q + 4, :].bitcast(I32))
        for q in range(4):
            nc.scalar.dma_start(w2s[32 * q : 32 * q + 8, :].bitcast(I32), w2_scales[:, 4 * q : 4 * q + 4, :].bitcast(I32))

        def load_w1(kp, rp):
            raw = slot(f"stage{kp}", f"w1raw{kp}{rp}", [P, PACK, HALF], F32)
            rows = w1[kp * PASS : (kp + 1) * PASS, rp * HALF : (rp + 1) * HALF]
            nc.sync.dma_start(raw[:], rows.rearrange("(p t) c -> p t c", t=PACK))
            return raw

        def load_w2(rp):
            words = held.tile([P, 2, HALF], U32, name=f"w2w{rp}", align_bytes=64)
            src = w2_words.rearrange("a p c i -> p a (c i)").bitcast(I32)
            nc.sync.dma_start(words[:].bitcast(I32), src[:, :, rp * HALF : (rp + 1) * HALF])
            return words

        def quantize_w1(raws, rp):
            made = []
            for kp in range(2):
                rounded = ring_rounded(("resp", "lin")[kp] + str(1 - rp))
                interleave(rounded[:], raws[kp][:])
                made.append(quantize(f"w1q{kp}{rp}", rounded))
            return made

        def load_page(rp, t):
            tile = held.tile([P, T2], F32, name=f"page{rp}{t}")
            rows = page0[rp * PASS : (rp + 1) * PASS, :].rearrange("(p t) c -> p t c", t=PACK)
            nc.sync.dma_start(tile[:], rows[:, t, :])
            return tile

        def load_wgs(name, start, count):
            tile = held.tile([P, PACK, count], F32, name=name)
            rows = wgs.rearrange("(c t) j -> c t j", t=PACK)
            for q in range(4):
                nc.sync.dma_start(tile[32 * q : 32 * q + 32, :, :], rows[:, :, start : start + count])
            return tile

        def load_ref(rp, half, tag):
            tile = slot(tag, f"ref{rp}{half}", [P, PACK, HALF], F32)
            rows = ref[rp * PASS : (rp + 1) * PASS, half * HALF : (half + 1) * HALF]
            nc.sync.dma_start(tile[:], rows.rearrange("(p t) m -> p t m", t=PACK))
            return tile

        w1raw = [load_w1(kp, 0) for kp in range(2)]
        load_table(1)
        w2w = [load_w2(0)]
        pages = {(0, t): load_page(0, t) for t in range(PACK)}

        wgs_first = held.tile([P, PACK, HALF], F32, name="wgs_first")
        wgs_turned = psum.tile([P, PACK, P], F32, name="turned")
        for u in range(PACK):
            nc.tensor.transpose(wgs_turned[:, u, :], wgs_rows[:, u * P : (u + 1) * P], ident[:])
        wgs_spread = slot("stage3", "wgs_spread", [P, PACK, PACK, 4, 32], F32)
        for q in range(4):
            nc.vector.tensor_copy(wgs_spread[:, :, :, q, :], wgs_turned[:].rearrange("j u (c t) -> j u t c", t=PACK))
        for t in range(PACK):
            back = psum.tile([P, HALF], F32, name="turned")
            for u in range(PACK):
                nc.tensor.transpose(back[:, u * P : (u + 1) * P], wgs_spread[:, u, t].rearrange("j q c -> j (q c)"), ident[:])
            nc.scalar.copy(wgs_first[:, t, :], back[:])
        wgs_parts = [wgs_first, load_wgs("wgs_second", HALF, HALF)]

        def wgs_cols(t, j0, count):
            return wgs_parts[j0 // HALF][:, t, j0 % HALF : j0 % HALF + count]

        vw = [held.tile([P, S], U32, name="vw0", align_bytes=64), order.tile([P, S], U32, name="vw1", offset=HALF * 4, align_bytes=64)]
        vs = held.tile([P, S], U8, name="vs", align_bytes=64)
        nc.vector.tensor_copy(vw[0][:], tabw[0][:].indirect(idx[:]))
        nc.vector.tensor_copy(vs[:], tabs[:].indirect(idx[:]))
        w1q = [quantize_w1(w1raw, 0)]
        for j0 in range(0, S, HALF):
            nc.vector.tensor_copy(vw[1][:, j0 : j0 + HALF], tabw[1][:].indirect(cols(idx, j0, HALF)))

        def product(jt, moving):
            bank = psum.tile([P, HALF], F32, name="bank")
            js = slice(jt * P, (jt + 1) * P)
            for kp in range(2):
                codes, scales = moving[kp]
                nc.tensor.matmul_mx(
                    out=bank[:], lhsT=vw[kp][:, js].bitcast(FP8X4), lhsT_scale=vs[4 * kp :, js],
                    rhs=codes.bitcast(FP8X4), rhs_scale=scales, start=(kp == 0), stop=(kp == 1),
                )
            return bank[:].rearrange("j (p t) -> j t p", t=PACK)

        def place(rp, j0, t, turned):
            h = ring.tile([P, CHUNK], F32, name="h", bufs=12)
            nc.scalar.activation(h[:], turned[:], ACT.Copy, scale=gains[:, rp, t : t + 1])
            window = pages[rp, t][:].indirect(cols(idx2, j0, CHUNK))
            nc.vector.tensor_tensor(window, h[:], wgs_cols(t, j0, CHUNK), ALU.mult)

        def update(step, rp, j0, waiting):
            w1_ops = [(c[:], s[:]) for c, s in w1q[rp]]
            w2_ops = [(w2w[rp][:, kp, :], w2s[4 * kp :, rp * HALF : (rp + 1) * HALF]) for kp in range(2)]
            a_banks = [product(j0 // P + u, w1_ops) for u in range(2)]
            b_banks = [product(j0 // P + u, w2_ops) for u in range(2)]
            resp = slot(f"resp{step % 2}", "resp", [P, PACK, 2, P], F32)
            lin = slot(f"lin{step % 2}", "lin", [P, PACK, 2, P], F32)
            if step < 2:
                for u in range(2):
                    nc.vector.tensor_copy(lin[:, :, u, :], b_banks[u])
            width = (1, 2, 2, 4, 4, 4, 4, 4)[step]
            left = []

            def place_one():
                if waiting:
                    place(*waiting.pop(0))

            for t0 in range(0, PACK, width):
                ts = slice(t0, t0 + width)
                flat = resp[:, ts].rearrange("j t u p -> j (t u p)")
                for u in range(2):
                    nc.scalar.activation(resp[:, ts, u, :], a_banks[u][:, ts, :], ACT.Square)
                place_one()
                if step >= 2:
                    nc.scalar.copy(lin[:, ts, 0, :], b_banks[0][:, ts, :])
                place_one()
                nc.scalar.activation(flat, flat, ACT.Abs_reciprocal_sqrt, bias=1.0)
                place_one()
                if step >= 2:
                    nc.scalar.copy(lin[:, ts, 1, :], b_banks[1][:, ts, :])
                place_one()
                nc.scalar.activation(flat, flat, ACT.Square)
                for t in range(t0, t0 + width):
                    turned = psum.tile([P, CHUNK], F32, name="turned")
                    for u in range(2):
                        dst = turned[:, u * P : (u + 1) * P]
                        nc.tensor.matmul(dst, lhsT=resp[:, t, u, :], rhs=ident[:], is_transpose=True, start=True, stop=False)
                        nc.tensor.matmul(dst, lhsT=lin[:, t, u, :], rhs=ident[:], is_transpose=True, start=False, stop=True)
                    if step in (4, 5, 6):
                        left.append((rp, j0, t, turned))
                    else:
                        place(rp, j0, t, turned)
            return left

        def recall(rp, half, refs, tag, width):
            diff = slot(tag, f"diff{rp}{half}", [P, PACK, HALF], F32)
            for m0 in range(0, HALF, width):
                for t in range(PACK):
                    window = pages[rp, t][:].indirect(cols(idx3, half * HALF + m0, width))
                    nc.vector.tensor_tensor(diff[:, t, m0 : m0 + width], window, refs[:, t, m0 : m0 + width], ALU.subtract)
            return diff

        def quantize_x(name, diff, rounded, width, codes):
            for m0 in range(0, HALF, width):
                interleave(rounded[:, m0 : m0 + width, :], diff[:, :, m0 : m0 + width])
            scales = held.tile([P, HALF], U8, name=name, align_bytes=64)
            nc.vector.quantize_mx(out=codes.bitcast(FP8X4), scales=scales[:], in_=rounded[:].rearrange("p w t -> p (w t)"))
            return codes, scales

        def score(half, nb, xq, y):
            bank = psum.tile([P, HALF], F32, name="bank")
            for rp in range(2):
                codes, scales = xq[rp]
                nc.tensor.matmul_mx(
                    out=bank[:], lhsT=w3w[:, rp, 2 * nb * P : 2 * (nb + 1) * P].bitcast(FP4X4),
                    lhsT_scale=w3s[:, rp, nb * P : (nb + 1) * P],
                    rhs=codes.bitcast(FP8X4), rhs_scale=scales[:], start=(rp == 0), stop=(rp == 1),
                )
            nc.scalar.activation(y, bank[:], ACT.Tanh)
            window = sheets[nb][:].indirect(cols(idx4, half * HALF, HALF))
            nc.vector.tensor_tensor(window, y, wgo_sb[:, half * HALF : (half + 1) * HALF], ALU.mult)

        def ring_y():
            return ring.tile([P, HALF], F32, name="y", bufs=2)[:]

        steps = [(rp, j0) for rp in range(2) for j0 in range(0, S, CHUNK)]
        xq = {}
        waiting = []
        for i, (rp, j0) in enumerate(steps):
            if i == 1:
                w1raw = [load_w1(kp, 1) for kp in range(2)]
                w2w.append(load_w2(1))
                ref00 = load_ref(0, 0, "stage2")
                ref01 = load_ref(0, 1, "stage4")
                for t in range(PACK):
                    pages[1, t] = load_page(1, t)
            if i == 4:
                w1q.append(quantize_w1(w1raw, 1))
                ref10 = load_ref(1, 0, "stage0")
                ref11 = load_ref(1, 1, "stage1")
                w3w = held.tile([P, 2, 2 * N], U8, name="w3w", align_bytes=64)
                nc.sync.dma_start(w3w[:].bitcast(I32), w3_words.rearrange("a p c -> p a c").bitcast(I32))
                for q in range(4):
                    src = w3_scales[:, 4 * q : 4 * q + 4, :].rearrange("a r n -> r a n")
                    nc.sync.dma_start(w3s[32 * q : 32 * q + 4, :, :].bitcast(I32), src.bitcast(I32))
            waiting = update(i, rp, j0, waiting)
            if i == 4:
                diff00 = recall(0, 0, ref00, "stage3", HALF)
                diff01 = recall(0, 1, ref01, "stage5", HALF)
                wgo_sb = held.tile([P, NP], F32, name="wgo_sb")
                nc.sync.dma_start(wgo_sb[:], wgo)
                sheets = []
                for nb in range(N // P):
                    sheet = shared.tile([P, T2], F32, name=f"sheet{nb}", offset=nb * T2 * 4)
                    nc.sync.dma_start(sheet[:], page1[nb * P : (nb + 1) * P, :])
                    sheets.append(sheet)

        diff10 = recall(1, 0, ref10, "stage2", CHUNK)
        first_codes = slot("stage0", "first_codes", [P, 2, HALF], U32)
        xq[0, 0] = quantize_x("xs00", diff00, ring_rounded("lin1"), HALF, first_codes[:, 0, :])
        xq[0, 1] = quantize_x("xs01", diff01, ring_rounded("resp1"), HALF, first_codes[:, 1, :])
        xq[1, 0] = quantize_x("xs10", diff10, ring_rounded("stage4"), CHUNK, slot("xq10", "xq10", [P, HALF], U32)[:])
        diff11 = recall(1, 1, ref11, "stage4", HALF)
        score(0, 0, [xq[0, 0], xq[1, 0]], slot("early", "y_early", [P, HALF], F32)[:])
        score(0, 1, [xq[0, 0], xq[1, 0]], ring_y())
        xq[1, 1] = quantize_x("xs11", diff11, ring_rounded("lin0"), HALF, slot("early", "xq11", [P, HALF], U32)[:])
        late = slot("stage4", "y_late", [P, 2, HALF], F32)
        for nb in range(2, 4):
            score(0, nb, [xq[0, 0], xq[1, 0]], late[:, nb - 2, :])
        for nb in range(4):
            score(1, nb, [xq[0, 1], xq[1, 1]], ring_y())
            nc.sync.dma_start(out[nb * P : (nb + 1) * P, :], sheets[nb][:])
